import numpy as np
import ml_dtypes


def mxq(x, axis, fmt="e4m3"):
    dtype, down = {"e4m3": (ml_dtypes.float8_e4m3fn, 7), "e5m2": (ml_dtypes.float8_e5m2, 14)}[fmt]
    v = np.moveaxis(np.asarray(x, np.float32).astype(ml_dtypes.bfloat16).astype(np.float64), axis, -1)
    blocks = v.reshape(v.shape[:-1] + (-1, 32))
    amax = np.abs(blocks).max(-1, keepdims=True)
    byte = np.maximum(np.where(amax > 0, np.frexp(amax)[1] - 1 + 127, 0) - down, 1)
    scale = np.exp2(byte - 127.0)
    codes = (blocks / scale).astype(np.float32).astype(dtype).astype(np.float64)
    return np.moveaxis((codes * scale).reshape(v.shape), -1, axis)


WIDE = False


def mx_kscale(k):
    if not WIDE:
        return np.ones(k)
    levels = np.array([10, -10, 5, -5, 0])
    if k % 512:
        return np.exp2(np.random.permutation(np.resize(levels, k // 32))).repeat(32)
    a = np.empty((k // 512, 16))
    for p in range(k // 512):
        a[p, :8] = np.random.permutation(np.resize(levels, 8))
        for g in range(8):
            far = levels[np.abs(levels - a[p, g]) >= 10]
            a[p, g + 8] = far[np.random.randint(len(far))]
    return np.exp2(a.ravel()).repeat(32)


def f64(x):
    return np.asarray(x).astype(np.float64)


def striped(idx):
    return np.tile(idx.reshape(-1, 16).T, (8, 1)).astype(np.uint16)


def unstriped(offs):
    return offs[:16].T.reshape(-1).astype(np.int64)


def striped8(idx):
    return np.concatenate([x.reshape(-1, 16).T for x in idx]).astype(np.uint16)


def runs(offs, k):
    lists = np.stack([offs[16 * r : 16 * r + 16].T.reshape(-1) for r in range(8)]).astype(np.int64)
    return lists[np.arange(k) % 512 // 64]


def pack_weight(w):
    k, n = w.shape
    w = f64(np.asarray(w, np.float32).astype(ml_dtypes.bfloat16)).reshape(k // 32, 32, n)
    amax = np.abs(w).max(1)
    byte = np.clip(np.where(amax > 0, np.frexp(amax)[1] - 1 + 127 - 7, 1), 1, 254)
    scaled = (w * np.exp2(127.0 - byte)[:, None, :]).reshape(k, n).astype(np.float32)
    words = np.ascontiguousarray(scaled.reshape(k // 512, 128, 4, n).transpose(0, 1, 3, 2)).astype(ml_dtypes.float8_e4m3fn).view(np.uint8)
    return words, np.ascontiguousarray(byte.astype(np.uint8).reshape(k // 512, 16, n))


def unpack_weight(words, scales):
    g, p, n, _ = words.shape
    vals = np.ascontiguousarray(words).view(ml_dtypes.float8_e4m3fn).astype(np.float64) * np.repeat(np.exp2(scales.astype(np.float64) - 127.0), 8, axis=1)[..., None]
    return vals.transpose(0, 1, 3, 2).reshape(g * 512, n)


def sigmoid(v):
    return 1.0 / (1.0 + np.exp(-np.maximum(v, -700.0)))

def planes(y):
    n, m = y.shape
    v = y.astype(np.float32).astype(ml_dtypes.bfloat16).astype(np.float64).reshape(n // 32, 32, m)
    top = np.abs(v).max(1)
    byte = np.clip(np.where(top > 0, np.frexp(top)[1] - 1 + 127 - 7, 1), 1, 254)
    codes = (v * np.exp2(127.0 - byte)[:, None, :]).reshape(n, m).astype(np.float32).astype(ml_dtypes.float8_e4m3fn).view(np.uint8)
    words = codes.reshape(n // 512, 128, 4, m).transpose(0, 1, 3, 2)
    return np.ascontiguousarray(words), np.ascontiguousarray(byte.astype(np.uint8).reshape(n // 512, 16, m))


K, T, S, N, H, C = 512, 2048, 512, 512, 512, 512


def setup_inputs():
    n = np.random.standard_normal
    s = mx_kscale(K)[:, None]
    u = mx_kscale(S)
    packed_xT = pack_weight(n((K, T)) * s)
    packed_w1 = pack_weight(n((K, H)) / np.sqrt(K) / s)
    packed_w2 = pack_weight(n((H, N)) / np.sqrt(H) / u[:, None])
    return {
        "x_words": packed_xT[0],
        "x_scales": packed_xT[1],
        "w1_words": packed_w1[0],
        "w1_scales": packed_w1[1],
        "sl": np.random.uniform(1.0, 2.0, (H, 1)).astype(np.float32),
        "th": (0.5 * n((H, 1))).astype(np.float32),
        "gn": (np.random.uniform(0.5, 1.5, (H, 1)) * u[:, None]).astype(np.float32),
        "w2_words": packed_w2[0],
        "w2_scales": packed_w2[1],
        "gs": (np.random.uniform(0.5, 1.5, (K, 1)) / s).astype(np.float32),
        "sl2": np.random.uniform(1.0, 2.0, (N, 1)).astype(np.float32),
        "th2": (0.5 * n((N, 1))).astype(np.float32),
        "sl3": np.random.uniform(1.0, 2.0, (C, 1)).astype(np.float32),
        "th3": (0.5 * n((C, 1))).astype(np.float32),
        "offs": striped(np.random.permutation(T)[:S]),
        "n1": striped8(np.stack([np.random.permutation(S) for _ in range(8)])),
        "n2": striped8(np.stack([np.random.permutation(S) for _ in range(8)])),
        "n3": striped8(np.stack([np.random.permutation(S) for _ in range(8)])),
        "n4": striped8(np.stack([np.random.permutation(S) for _ in range(8)])),
        "cand": striped(np.random.permutation(T)[:C]),
        "n5": striped8(np.stack([np.random.permutation(S) for _ in range(8)])),
        "n6": striped8(np.stack([np.random.permutation(S) for _ in range(8)])),
    }


def reference(x_words, x_scales, w1_words, w1_scales, sl, th, gn, w2_words, w2_scales, gs, sl2, th2, sl3, th3, offs, n1, n2, n3, n4, cand, n5, n6):
    xq = unpack_weight(x_words, x_scales)[:, unstriped(offs)]
    y = unpack_weight(w1_words, w1_scales).T @ xq
    z = f64(gn) * ((y - (y[np.arange(H)[:, None], runs(n1, H)])) * (sigmoid(y[np.arange(H)[:, None], runs(n2, H)])))
    a = unpack_weight(w2_words, w2_scales).T @ mxq(z, 0, "e4m3")
    sg2 = sigmoid(f64(sl2) * (a[np.arange(N)[:, None], runs(n5, N)] - f64(th2)))
    x_cand = unpack_weight(x_words, x_scales)[:, unstriped(cand)]
    pa = y[np.arange(H)[:, None], runs(n3, H)]
    sg = sigmoid(f64(sl) * (y[np.arange(H)[:, None], runs(n4, H)] - f64(th)))
    z2 = f64(gs) * (pa + sg * (y - pa))
    b = 0.0625 * ((x_cand.T @ mxq(z2, 0, "e4m3")))
    sg3 = sigmoid(f64(sl3) * (b[np.arange(C)[:, None], runs(n6, C)] - f64(th3)))
    out_0 = sg2 * b + sg3 * a
    return (out_0,) + planes(out_0)

@@ -1,0 +1,218 @@
+from contextlib import ExitStack
+
+import concourse.mybir as mybir
+
+K, T, S = 512, 2048, 512
+FLOPS = 3 * 2 * K * S * S
+
+F32 = mybir.dt.float32
+BF16 = mybir.dt.bfloat16
+I32 = mybir.dt.int32
+U32 = mybir.dt.uint32
+U16 = mybir.dt.uint16
+U8 = mybir.dt.uint8
+FP8X4 = mybir.dt.float8_e4m3fn_x4
+ALU = mybir.AluOpType
+ACT = mybir.ActivationFunctionType
+
+P = 128
+PACK = 4
+HALF = S // 2
+WINDOW = 2 * S
+
+
+def tile_picked_fkcdcxbgdifebl_none_po_kernel(
+    tc, x_words, x_scales, w1_words, w1_scales, sl, th, gn, w2_words, w2_scales, gs, sl2, th2, sl3, th3,
+    offs, n1, n2, n3, n4, cand, n5, n6, out_0, out_1, out_2,
+):
+    nc = tc.nc
+    with ExitStack() as ctx:
+        keep = ctx.enter_context(tc.tile_pool(name="keep", bufs=1))
+        psum = ctx.enter_context(tc.psum_pool(name="psum", bufs=1))
+
+        def load_list(name, src):
+            lst = keep.tile([P, S // 16], U16, name=name)
+            nc.sync.dma_start(lst[:], src)
+            return lst
+
+        def load_words(queue, name, src, width):
+            words = keep.tile([P, width], I32, name=name, align_bytes=64)
+            queue.dma_start(words[:], src[0].rearrange("p c r -> p (c r)").bitcast(I32))
+            return words
+
+        def load_scales(queue, zeroing, name, src, width):
+            plane = keep.tile([P, width], U8, name=name, align_bytes=64)
+            zeroing.memset(plane[:].bitcast(I32), 0)
+            for q in range(4):
+                queue.dma_start(plane[32 * q : 32 * q + 4, :].bitcast(I32), src[0, 4 * q : 4 * q + 4, :].bitcast(I32))
+            return plane
+
+        def load_rows(queue, name, src):
+            vec = keep.tile([P, PACK], F32, name=name)
+            queue.dma_start(vec[:], src.rearrange("(p t) o -> p (t o)", t=PACK))
+            return vec
+
+        def negated_product(name, u, v):
+            prod = keep.tile([P, PACK], F32, name=name + "_pos")
+            nc.gpsimd.tensor_tensor(prod[:], u[:], v[:], ALU.mult)
+            return negated(name, prod)
+
+        def negated(name, u):
+            neg = keep.tile([P, PACK], F32, name=name)
+            nc.gpsimd.tensor_scalar(neg[:], u[:], -1.0, 0.0, ALU.mult, ALU.add)
+            return neg
+
+        def dealt_read(ap):
+            return ap.rearrange("p (m t) -> p t m", t=PACK)
+
+        def dealt_tile(ap):
+            return ap.rearrange("p (t m) -> p t m", t=PACK)
+
+        def dealt_write(ap):
+            return ap.rearrange("p (t m) -> p m t", t=PACK)
+
+        def planes_view(quad, h):
+            return quad[:, :, h * HALF : (h + 1) * HALF].rearrange("p t (c i) -> p c t i", i=4)
+
+        def woven_view(woven, h):
+            return woven[:, h * PACK * HALF : (h + 1) * PACK * HALF].rearrange("p (c i t) -> p c t i", i=4, t=PACK)
+
+        def quantise(codes, scales, woven, h):
+            cols = slice(h * HALF, (h + 1) * HALF)
+            nc.vector.quantize_mx(out=codes[:, cols].bitcast(FP8X4), scales=scales[:, cols], in_=woven[:, h * PACK * HALF : (h + 1) * PACK * HALF])
+
+        def product(bank, lhs_codes, lhs_scales, t, rhs_codes, rhs_scales, cols):
+            rows = slice(t * P, (t + 1) * P)
+            nc.tensor.matmul_mx(
+                out=bank[:, cols], lhsT=lhs_codes[:, rows].bitcast(FP8X4), lhsT_scale=lhs_scales[:, rows],
+                rhs=rhs_codes[:, cols].bitcast(FP8X4), rhs_scale=rhs_scales[:, cols], start=True, stop=True,
+            )
+
+        x_w = load_words(nc.sync, "x_w", x_words, T)
+        offs_l = load_list("offs_l", offs)
+        x_s = load_scales(nc.sync, nc.vector, "x_s", x_scales, T)
+        w1_w = load_words(nc.scalar, "w1_w", w1_words, S)
+        w1_s = load_scales(nc.scalar, nc.vector, "w1_s", w1_scales, S)
+        cand_l = load_list("cand_l", cand)
+        n4_l = load_list("n4_l", n4)
+        sl_v = load_rows(nc.sync, "sl_v", sl)
+        th_v = load_rows(nc.sync, "th_v", th)
+        gs_v = load_rows(nc.sync, "gs_v", gs)
+        bias1 = keep.tile([P, PACK], F32, name="bias1")
+        nc.vector.scalar_tensor_tensor(bias1[:], sl_v[:], -1.0, th_v[:], ALU.mult, ALU.mult)
+        n3_l = load_list("n3_l", n3)
+        n2_l = load_list("n2_l", n2)
+        n1_l = load_list("n1_l", n1)
+        w2_w = load_words(nc.sync, "w2_w", w2_words, S)
+        n6_l = load_list("n6_l", n6)
+        n5_l = load_list("n5_l", n5)
+        gn_v = load_rows(nc.gpsimd, "gn_v", gn)
+        neg_gn = keep.tile([P, PACK], F32, name="neg_gn")
+        nc.vector.tensor_scalar(neg_gn[:], gn_v[:], -1.0, 0.0, ALU.mult, ALU.add)
+        w2_s = load_scales(nc.gpsimd, nc.gpsimd, "w2_s", w2_scales, S)
+        sl3_v = load_rows(nc.gpsimd, "sl3_v", sl3)
+        th3_v = load_rows(nc.gpsimd, "th3_v", th3)
+        sl2_v = load_rows(nc.gpsimd, "sl2_v", sl2)
+        th2_v = load_rows(nc.gpsimd, "th2_v", th2)
+        bias3 = negated_product("bias3", sl3_v, th3_v)
+        bias2 = negated_product("bias2", sl2_v, th2_v)
+
+        pick_s = keep.tile([P, S], U8, name="pick_s", align_bytes=64)
+        nc.vector.tensor_copy(pick_s[:], x_s[:].indirect(offs_l[:]))
+        w1_sd = keep.tile([P, S], U8, name="w1_sd", align_bytes=64)
+        nc.vector.tensor_copy(dealt_tile(w1_sd[:]), dealt_read(w1_s[:]))
+        w1_wd = keep.tile([P, S], U32, name="w1_wd", align_bytes=64)
+        nc.scalar.copy(dealt_tile(w1_wd[:]), dealt_read(w1_w[:].bitcast(U32)))
+        pick_w = keep.tile([P, S], U32, name="pick_w", align_bytes=64)
+        nc.vector.tensor_copy(pick_w[:], x_w[:].bitcast(U32).indirect(offs_l[:]))
+        cand_s = keep.tile([P, S], U8, name="cand_s", align_bytes=64)
+        nc.vector.tensor_copy(dealt_write(cand_s[:]), x_s[:].indirect(cand_l[:]))
+        cand_w = keep.tile([P, S], U32, name="cand_w", align_bytes=64)
+        nc.vector.tensor_copy(dealt_write(cand_w[:]), x_w[:].bitcast(U32).indirect(cand_l[:]))
+
+        y_bank = [psum.tile([P, S], F32, name="y_bank%d" % t, tag="first%d" % t) for t in range(PACK)]
+        y_win = [keep.tile([P, WINDOW], F32, name="y_win%d" % t) for t in range(PACK)]
+        y_plain = [keep.tile([P, S], F32, name="y_plain%d" % t) for t in range(PACK)]
+        sg = keep.tile([P, PACK, S], F32, name="sg")
+        keep_pa = keep.tile([P, PACK, S], F32, name="keep_pa")
+        from_pa = keep.tile([P, PACK, S], F32, name="from_pa")
+        from_y = keep.tile([P, PACK, S], F32, name="from_y")
+        for t in range(PACK):
+            product(y_bank[t], w1_wd, w1_sd, t, pick_w, pick_s, slice(0, S))
+        for t in range(PACK):
+            col = slice(t, t + 1)
+            nc.scalar.activation(y_win[t][:, 0:S], y_bank[t][:], ACT.Copy)
+            nc.sync.dma_start(y_plain[t][:], y_win[t][:, 0:S])
+            nc.scalar.activation(sg[:, t, :], y_win[t][:].indirect(n4_l[:]), ACT.Sigmoid, bias=bias1[:, col], scale=sl_v[:, col])
+            nc.vector.tensor_scalar(keep_pa[:, t, :], sg[:, t, :], 1.0, gs_v[:, col], ALU.subtract, ALU.mult)
+            nc.vector.scalar_tensor_tensor(from_y[:, t, :], sg[:, t, :], gs_v[:, col], y_bank[t][:], ALU.mult, ALU.mult)
+            nc.vector.tensor_tensor(from_pa[:, t, :], y_win[t][:].indirect(n3_l[:]), keep_pa[:, t, :], ALU.mult)
+        z2_woven = keep.tile([P, PACK * S], BF16, name="z2_woven", align_bytes=64)
+        z2_w = keep.tile([P, S], U32, name="z2_w", align_bytes=64)
+        z2_s = keep.tile([P, S], U8, name="z2_s", align_bytes=64)
+        b_bank = [psum.tile([P, S], F32, name="b_bank%d" % t) for t in range(PACK)]
+        for h in range(2):
+            nc.vector.tensor_tensor(woven_view(z2_woven, h), planes_view(from_y, h), planes_view(from_pa, h), ALU.subtract)
+        for h in range(2):
+            quantise(z2_w, z2_s, z2_woven, h)
+            for t in range(PACK):
+                product(b_bank[t], cand_w, cand_s, t, z2_w, z2_s, slice(h * HALF, (h + 1) * HALF))
+
+        gate = keep.tile([P, PACK, S], F32, name="gate")
+        gain = keep.tile([P, PACK, S], F32, name="gain")
+        diff = keep.tile([P, PACK, S], F32, name="diff")
+        for t in range(PACK):
+            nc.scalar.activation(gate[:, t, :], y_win[t][:].indirect(n2_l[:]), ACT.Sigmoid)
+        for t in range(PACK):
+            nc.scalar.activation(gain[:, t, :], gate[:, t, :], ACT.Copy, scale=neg_gn[:, t : t + 1])
+        w2_wd = keep.tile([P, S], U32, name="w2_wd", align_bytes=64)
+        nc.scalar.copy(dealt_tile(w2_wd[:]), dealt_read(w2_w[:].bitcast(U32)))
+        w2_sd = keep.tile([P, S], U8, name="w2_sd", align_bytes=64)
+        nc.gpsimd.tensor_copy(dealt_tile(w2_sd[:]), dealt_read(w2_s[:]))
+        for t in range(PACK):
+            nc.vector.tensor_tensor(diff[:, t, :], y_win[t][:].indirect(n1_l[:]), y_plain[t][:], ALU.subtract)
+        z_woven = keep.tile([P, PACK * S], BF16, name="z_woven", align_bytes=64)
+        z_w = keep.tile([P, S], U32, name="z_w", align_bytes=64)
+        z_s = keep.tile([P, S], U8, name="z_s", align_bytes=64)
+        a_bank = [psum.tile([P, S], F32, name="a_bank%d" % t, tag="first%d" % t) for t in range(PACK)]
+        for h in range(2):
+            nc.vector.tensor_tensor(woven_view(z_woven, h), planes_view(diff, h), planes_view(gain, h), ALU.mult)
+        for h in range(2):
+            quantise(z_w, z_s, z_woven, h)
+            for t in range(PACK):
+                product(a_bank[t], w2_wd, w2_sd, t, z_w, z_s, slice(h * HALF, (h + 1) * HALF))
+
+        b_win = [keep.tile([P, WINDOW], F32, name="b_win%d" % t) for t in range(PACK)]
+        sg3 = keep.tile([P, PACK, S], F32, name="sg3")
+        for t in range(PACK):
+            col = slice(t, t + 1)
+            nc.scalar.activation(b_win[t][:, 0:S], b_bank[t][:], ACT.Copy, scale=0.0625)
+            nc.scalar.activation(sg3[:, t, :], b_win[t][:].indirect(n6_l[:]), ACT.Sigmoid, bias=bias3[:, col], scale=sl3_v[:, col])
+
+        a_win = [keep.tile([P, WINDOW], F32, name="a_win%d" % t) for t in range(PACK)]
+        sg2 = keep.tile([P, PACK, S], F32, name="sg2")
+        term_a = keep.tile([P, PACK, S], F32, name="term_a")
+        term_b = keep.tile([P, PACK, S], F32, name="term_b")
+        result = keep.tile([P, PACK, S], F32, name="result")
+        out_woven = keep.tile([P, PACK * S], BF16, name="out_woven", align_bytes=64)
+        out_w = keep.tile([P, S], U32, name="out_w", align_bytes=64)
+        out_s = keep.tile([P, S], U8, name="out_s", align_bytes=64)
+        for t in range(PACK):
+            nc.scalar.activation(a_win[t][:, 0:S], a_bank[t][:], ACT.Copy)
+            nc.vector.tensor_tensor(term_a[:, t, :], sg3[:, t, :], a_bank[t][:], ALU.mult)
+        out_rows = out_0.rearrange("(p t) j -> p t j", t=PACK)
+        out_words = out_1[0].rearrange("p c r -> p (c r)").bitcast(I32)
+        for h in range(2):
+            cols = slice(h * HALF, (h + 1) * HALF)
+            for t in range(PACK):
+                col = slice(t, t + 1)
+                nc.scalar.activation(sg2[:, t, cols], a_win[t][:].indirect(n5_l[:, h * HALF // 16 : (h + 1) * HALF // 16]), ACT.Sigmoid, bias=bias2[:, col], scale=sl2_v[:, col])
+                nc.vector.tensor_tensor(term_b[:, t, cols], sg2[:, t, cols], b_win[t][:, cols], ALU.mult)
+            nc.vector.tensor_tensor(result[:, :, cols], term_a[:, :, cols], term_b[:, :, cols], ALU.add)
+            nc.sync.dma_start(out_rows[:, :, cols], result[:, :, cols])
+            nc.vector.tensor_copy(woven_view(out_woven, h), planes_view(result, h))
+            quantise(out_w, out_s, out_woven, h)
+            nc.sync.dma_start(out_words[:, cols], out_w[:, cols].bitcast(I32))
+        for q in range(4):
+            queue = nc.sync if q % 2 == 0 else nc.scalar
+            queue.dma_start(out_2[0, 4 * q : 4 * q + 4, :].bitcast(I32), out_s[32 * q : 32 * q + 4, :].bitcast(I32))

@@ -53,13 +53,8 @@ def tile_picked_fkcdcxbgdifebl_none_po_kernel(
             return vec
 
         def negated_product(name, u, v):
-            prod = keep.tile([P, PACK], F32, name=name + "_pos")
-            nc.gpsimd.tensor_tensor(prod[:], u[:], v[:], ALU.mult)
-            return negated(name, prod)
-
-        def negated(name, u):
             neg = keep.tile([P, PACK], F32, name=name)
-            nc.gpsimd.tensor_scalar(neg[:], u[:], -1.0, 0.0, ALU.mult, ALU.add)
+            nc.vector.scalar_tensor_tensor(neg[:], u[:], -1.0, v[:], ALU.mult, ALU.mult)
             return neg
 
         def dealt_read(ap):
@@ -72,10 +67,10 @@ def tile_picked_fkcdcxbgdifebl_none_po_kernel(
             return ap.rearrange("p (t m) -> p m t", t=PACK)
 
         def planes_view(quad, h):
-            return quad[:, :, h * HALF : (h + 1) * HALF].rearrange("p t (c i) -> p c t i", i=4)
+            return quad[:, :, h * HALF : (h + 1) * HALF].rearrange("p t (c i) -> p c t i", i=2)
 
         def woven_view(woven, h):
-            return woven[:, h * PACK * HALF : (h + 1) * PACK * HALF].rearrange("p (c i t) -> p c t i", i=4, t=PACK)
+            return woven[:, h * PACK * HALF : (h + 1) * PACK * HALF].rearrange("p (c i t) -> p c t i", i=2, t=PACK)
 
         def quantise(codes, scales, woven, h):
             cols = slice(h * HALF, (h + 1) * HALF)
@@ -88,32 +83,31 @@ def tile_picked_fkcdcxbgdifebl_none_po_kernel(
                 rhs=rhs_codes[:, cols].bitcast(FP8X4), rhs_scale=rhs_scales[:, cols], start=True, stop=True,
             )
 
-        x_w = load_words(nc.sync, "x_w", x_words, T)
         offs_l = load_list("offs_l", offs)
-        x_s = load_scales(nc.sync, nc.vector, "x_s", x_scales, T)
-        w1_w = load_words(nc.scalar, "w1_w", w1_words, S)
-        w1_s = load_scales(nc.scalar, nc.vector, "w1_s", w1_scales, S)
         cand_l = load_list("cand_l", cand)
+        x_w = load_words(nc.sync, "x_w", x_words, T)
+        w1_w = load_words(nc.scalar, "w1_w", w1_words, S)
+        x_s = load_scales(nc.scalar, nc.vector, "x_s", x_scales, T)
+        w1_s = load_scales(nc.gpsimd, nc.gpsimd, "w1_s", w1_scales, S)
+        w2_w = load_words(nc.sync, "w2_w", w2_words, S)
         n4_l = load_list("n4_l", n4)
         sl_v = load_rows(nc.sync, "sl_v", sl)
         th_v = load_rows(nc.sync, "th_v", th)
-        gs_v = load_rows(nc.sync, "gs_v", gs)
-        bias1 = keep.tile([P, PACK], F32, name="bias1")
-        nc.vector.scalar_tensor_tensor(bias1[:], sl_v[:], -1.0, th_v[:], ALU.mult, ALU.mult)
         n3_l = load_list("n3_l", n3)
-        n2_l = load_list("n2_l", n2)
-        n1_l = load_list("n1_l", n1)
-        w2_w = load_words(nc.sync, "w2_w", w2_words, S)
-        n6_l = load_list("n6_l", n6)
-        n5_l = load_list("n5_l", n5)
+        gs_v = load_rows(nc.gpsimd, "gs_v", gs)
         gn_v = load_rows(nc.gpsimd, "gn_v", gn)
+        bias1 = negated_product("bias1", sl_v, th_v)
         neg_gn = keep.tile([P, PACK], F32, name="neg_gn")
         nc.vector.tensor_scalar(neg_gn[:], gn_v[:], -1.0, 0.0, ALU.mult, ALU.add)
+        n2_l = load_list("n2_l", n2)
+        n1_l = load_list("n1_l", n1)
+        n6_l = load_list("n6_l", n6)
+        n5_l = load_list("n5_l", n5)
         w2_s = load_scales(nc.gpsimd, nc.gpsimd, "w2_s", w2_scales, S)
-        sl3_v = load_rows(nc.gpsimd, "sl3_v", sl3)
-        th3_v = load_rows(nc.gpsimd, "th3_v", th3)
-        sl2_v = load_rows(nc.gpsimd, "sl2_v", sl2)
-        th2_v = load_rows(nc.gpsimd, "th2_v", th2)
+        sl3_v = load_rows(nc.sync, "sl3_v", sl3)
+        th3_v = load_rows(nc.sync, "th3_v", th3)
+        sl2_v = load_rows(nc.sync, "sl2_v", sl2)
+        th2_v = load_rows(nc.sync, "th2_v", th2)
         bias3 = negated_product("bias3", sl3_v, th3_v)
         bias2 = negated_product("bias2", sl2_v, th2_v)
 
@@ -123,6 +117,8 @@ def tile_picked_fkcdcxbgdifebl_none_po_kernel(
         nc.vector.tensor_copy(dealt_tile(w1_sd[:]), dealt_read(w1_s[:]))
         w1_wd = keep.tile([P, S], U32, name="w1_wd", align_bytes=64)
         nc.scalar.copy(dealt_tile(w1_wd[:]), dealt_read(w1_w[:].bitcast(U32)))
+        w2_wd = keep.tile([P, S], U32, name="w2_wd", align_bytes=64)
+        nc.scalar.copy(dealt_tile(w2_wd[:]), dealt_read(w2_w[:].bitcast(U32)))
         pick_w = keep.tile([P, S], U32, name="pick_w", align_bytes=64)
         nc.vector.tensor_copy(pick_w[:], x_w[:].bitcast(U32).indirect(offs_l[:]))
         cand_s = keep.tile([P, S], U8, name="cand_s", align_bytes=64)
@@ -163,14 +159,13 @@ def tile_picked_fkcdcxbgdifebl_none_po_kernel(
         diff = keep.tile([P, PACK, S], F32, name="diff")
         for t in range(PACK):
             nc.scalar.activation(gate[:, t, :], y_win[t][:].indirect(n2_l[:]), ACT.Sigmoid)
-        for t in range(PACK):
+        for t in range(PACK - 1):
             nc.scalar.activation(gain[:, t, :], gate[:, t, :], ACT.Copy, scale=neg_gn[:, t : t + 1])
-        w2_wd = keep.tile([P, S], U32, name="w2_wd", align_bytes=64)
-        nc.scalar.copy(dealt_tile(w2_wd[:]), dealt_read(w2_w[:].bitcast(U32)))
         w2_sd = keep.tile([P, S], U8, name="w2_sd", align_bytes=64)
-        nc.gpsimd.tensor_copy(dealt_tile(w2_sd[:]), dealt_read(w2_s[:]))
+        nc.vector.tensor_copy(dealt_tile(w2_sd[:]), dealt_read(w2_s[:]))
         for t in range(PACK):
             nc.vector.tensor_tensor(diff[:, t, :], y_win[t][:].indirect(n1_l[:]), y_plain[t][:], ALU.subtract)
+        nc.vector.tensor_scalar(gain[:, 3, :], gate[:, 3, :], neg_gn[:, 3:4], 0.0, ALU.mult, ALU.add)
         z_woven = keep.tile([P, PACK * S], BF16, name="z_woven", align_bytes=64)
         z_w = keep.tile([P, S], U32, name="z_w", align_bytes=64)
         z_s = keep.tile([P, S], U8, name="z_s", align_bytes=64)

@@ -35,8 +35,8 @@ def tile_picked_fkcdcxbgdifebl_none_po_kernel(
             nc.sync.dma_start(lst[:], src)
             return lst
 
-        def load_words(queue, name, src, width):
-            words = keep.tile([P, width], I32, name=name, align_bytes=64)
+        def load_words(queue, name, tag, src, width):
+            words = keep.tile([P, width], I32, name=name, tag=tag, align_bytes=64)
             queue.dma_start(words[:], src[0].rearrange("p c r -> p (c r)").bitcast(I32))
             return words
 
@@ -47,8 +47,8 @@ def tile_picked_fkcdcxbgdifebl_none_po_kernel(
                 queue.dma_start(plane[32 * q : 32 * q + 4, :].bitcast(I32), src[0, 4 * q : 4 * q + 4, :].bitcast(I32))
             return plane
 
-        def load_rows(queue, name, src):
-            vec = keep.tile([P, PACK], F32, name=name)
+        def load_rows(queue, name, tag, src):
+            vec = keep.tile([P, PACK], F32, name=name, tag=tag)
             queue.dma_start(vec[:], src.rearrange("(p t) o -> p (t o)", t=PACK))
             return vec
 
@@ -84,41 +84,37 @@ def tile_picked_fkcdcxbgdifebl_none_po_kernel(
             )
 
         offs_l = load_list("offs_l", offs)
-        cand_l = load_list("cand_l", cand)
-        x_w = load_words(nc.sync, "x_w", x_words, T)
-        w1_w = load_words(nc.scalar, "w1_w", w1_words, S)
-        x_s = load_scales(nc.scalar, nc.vector, "x_s", x_scales, T)
-        w1_s = load_scales(nc.gpsimd, nc.gpsimd, "w1_s", w1_scales, S)
-        w2_w = load_words(nc.sync, "w2_w", w2_words, S)
+        w1_w = load_words(nc.scalar, "w1_w", "w_words", w1_words, S)
         n4_l = load_list("n4_l", n4)
-        sl_v = load_rows(nc.sync, "sl_v", sl)
-        th_v = load_rows(nc.sync, "th_v", th)
         n3_l = load_list("n3_l", n3)
-        gs_v = load_rows(nc.gpsimd, "gs_v", gs)
-        gn_v = load_rows(nc.gpsimd, "gn_v", gn)
-        bias1 = negated_product("bias1", sl_v, th_v)
-        neg_gn = keep.tile([P, PACK], F32, name="neg_gn")
-        nc.vector.tensor_scalar(neg_gn[:], gn_v[:], -1.0, 0.0, ALU.mult, ALU.add)
         n2_l = load_list("n2_l", n2)
         n1_l = load_list("n1_l", n1)
+        x_w = load_words(nc.sync, "x_w", "x_words", x_words, T)
+        cand_l = load_list("cand_l", cand)
         n6_l = load_list("n6_l", n6)
         n5_l = load_list("n5_l", n5)
-        w2_s = load_scales(nc.gpsimd, nc.gpsimd, "w2_s", w2_scales, S)
-        sl3_v = load_rows(nc.sync, "sl3_v", sl3)
-        th3_v = load_rows(nc.sync, "th3_v", th3)
-        sl2_v = load_rows(nc.sync, "sl2_v", sl2)
-        th2_v = load_rows(nc.sync, "th2_v", th2)
-        bias3 = negated_product("bias3", sl3_v, th3_v)
-        bias2 = negated_product("bias2", sl2_v, th2_v)
+        x_s = load_scales(nc.scalar, nc.vector, "x_s", x_scales, T)
+        w2_s = load_scales(nc.sync, nc.vector, "w2_s", w2_scales, S)
+        w1_s = load_scales(nc.scalar, nc.vector, "w1_s", w1_scales, S)
+        sl_v = load_rows(nc.gpsimd, "sl_v", "slope", sl)
+        th_v = load_rows(nc.gpsimd, "th_v", "threshold", th)
+        gs_v = load_rows(nc.gpsimd, "gs_v", "weight", gs)
+        gn_v = load_rows(nc.gpsimd, "gn_v", "gain", gn)
 
         pick_s = keep.tile([P, S], U8, name="pick_s", align_bytes=64)
         nc.vector.tensor_copy(pick_s[:], x_s[:].indirect(offs_l[:]))
-        w1_sd = keep.tile([P, S], U8, name="w1_sd", align_bytes=64)
-        nc.vector.tensor_copy(dealt_tile(w1_sd[:]), dealt_read(w1_s[:]))
+        w1_sd = keep.tile([P, S], U8, name="w1_sd", tag="w_sd", align_bytes=64)
+        for t in range(PACK):
+            nc.gpsimd.tensor_copy(dealt_tile(w1_sd[:])[:, t, :], dealt_read(w1_s[:])[:, t, :])
         w1_wd = keep.tile([P, S], U32, name="w1_wd", align_bytes=64)
         nc.scalar.copy(dealt_tile(w1_wd[:]), dealt_read(w1_w[:].bitcast(U32)))
-        w2_wd = keep.tile([P, S], U32, name="w2_wd", align_bytes=64)
-        nc.scalar.copy(dealt_tile(w2_wd[:]), dealt_read(w2_w[:].bitcast(U32)))
+        w2_w = load_words(nc.sync, "w2_w", "w_words", w2_words, S)
+        neg_th = keep.tile([P, PACK], F32, name="neg_th")
+        nc.gpsimd.tensor_scalar(neg_th[:], th_v[:], -1.0, 0.0, ALU.mult, ALU.add)
+        bias1 = keep.tile([P, PACK], F32, name="bias1")
+        nc.gpsimd.tensor_tensor(bias1[:], neg_th[:], sl_v[:], ALU.mult)
+        neg_gn = keep.tile([P, PACK], F32, name="neg_gn")
+        nc.gpsimd.tensor_scalar(neg_gn[:], gn_v[:], -1.0, 0.0, ALU.mult, ALU.add)
         pick_w = keep.tile([P, S], U32, name="pick_w", align_bytes=64)
         nc.vector.tensor_copy(pick_w[:], x_w[:].bitcast(U32).indirect(offs_l[:]))
         cand_s = keep.tile([P, S], U8, name="cand_s", align_bytes=64)
@@ -131,7 +127,7 @@ def tile_picked_fkcdcxbgdifebl_none_po_kernel(
         y_plain = [keep.tile([P, S], F32, name="y_plain%d" % t) for t in range(PACK)]
         sg = keep.tile([P, PACK, S], F32, name="sg")
         keep_pa = keep.tile([P, PACK, S], F32, name="keep_pa")
-        from_pa = keep.tile([P, PACK, S], F32, name="from_pa")
+        from_pa = keep.tile([P, PACK, S], F32, name="from_pa", tag="gathered")
         from_y = keep.tile([P, PACK, S], F32, name="from_y")
         for t in range(PACK):
             product(y_bank[t], w1_wd, w1_sd, t, pick_w, pick_s, slice(0, S))
@@ -143,6 +139,12 @@ def tile_picked_fkcdcxbgdifebl_none_po_kernel(
             nc.vector.tensor_scalar(keep_pa[:, t, :], sg[:, t, :], 1.0, gs_v[:, col], ALU.subtract, ALU.mult)
             nc.vector.scalar_tensor_tensor(from_y[:, t, :], sg[:, t, :], gs_v[:, col], y_bank[t][:], ALU.mult, ALU.mult)
             nc.vector.tensor_tensor(from_pa[:, t, :], y_win[t][:].indirect(n3_l[:]), keep_pa[:, t, :], ALU.mult)
+        sl3_v = load_rows(nc.sync, "sl3_v", "slope", sl3)
+        th3_v = load_rows(nc.sync, "th3_v", "threshold", th3)
+        bias3 = negated_product("bias3", sl3_v, th3_v)
+        sl2_v = load_rows(nc.sync, "sl2_v", "weight", sl2)
+        th2_v = load_rows(nc.sync, "th2_v", "threshold", th2)
+        bias2 = negated_product("bias2", sl2_v, th2_v)
         z2_woven = keep.tile([P, PACK * S], BF16, name="z2_woven", align_bytes=64)
         z2_w = keep.tile([P, S], U32, name="z2_w", align_bytes=64)
         z2_s = keep.tile([P, S], U8, name="z2_s", align_bytes=64)
@@ -156,16 +158,17 @@ def tile_picked_fkcdcxbgdifebl_none_po_kernel(
 
         gate = keep.tile([P, PACK, S], F32, name="gate")
         gain = keep.tile([P, PACK, S], F32, name="gain")
-        diff = keep.tile([P, PACK, S], F32, name="diff")
+        diff = keep.tile([P, PACK, S], F32, name="diff", tag="gathered")
         for t in range(PACK):
             nc.scalar.activation(gate[:, t, :], y_win[t][:].indirect(n2_l[:]), ACT.Sigmoid)
-        for t in range(PACK - 1):
+        for t in range(PACK):
             nc.scalar.activation(gain[:, t, :], gate[:, t, :], ACT.Copy, scale=neg_gn[:, t : t + 1])
-        w2_sd = keep.tile([P, S], U8, name="w2_sd", align_bytes=64)
+        w2_wd = keep.tile([P, S], U32, name="w2_wd", align_bytes=64)
+        nc.gpsimd.tensor_copy(dealt_tile(w2_wd[:]), dealt_read(w2_w[:].bitcast(U32)))
+        w2_sd = keep.tile([P, S], U8, name="w2_sd", tag="w_sd", align_bytes=64)
         nc.vector.tensor_copy(dealt_tile(w2_sd[:]), dealt_read(w2_s[:]))
         for t in range(PACK):
             nc.vector.tensor_tensor(diff[:, t, :], y_win[t][:].indirect(n1_l[:]), y_plain[t][:], ALU.subtract)
-        nc.vector.tensor_scalar(gain[:, 3, :], gate[:, 3, :], neg_gn[:, 3:4], 0.0, ALU.mult, ALU.add)
         z_woven = keep.tile([P, PACK * S], BF16, name="z_woven", align_bytes=64)
         z_w = keep.tile([P, S], U32, name="z_w", align_bytes=64)
         z_s = keep.tile([P, S], U8, name="z_s", align_bytes=64)
@@ -193,19 +196,29 @@ def tile_picked_fkcdcxbgdifebl_none_po_kernel(
         out_w = keep.tile([P, S], U32, name="out_w", align_bytes=64)
         out_s = keep.tile([P, S], U8, name="out_s", align_bytes=64)
         for t in range(PACK):
-            nc.scalar.activation(a_win[t][:, 0:S], a_bank[t][:], ACT.Copy)
-            nc.vector.tensor_tensor(term_a[:, t, :], sg3[:, t, :], a_bank[t][:], ALU.mult)
+            if t % 2 == 0:
+                nc.scalar.activation(a_win[t][:, 0:S], a_bank[t][:], ACT.Copy)
+            else:
+                nc.vector.tensor_copy(a_win[t][:, 0:S], a_bank[t][:])
+        for t in range(PACK):
+            if t % 2 == 0:
+                nc.gpsimd.tensor_tensor(term_a[:, t, :], sg3[:, t, :], a_win[t][:, 0:S], ALU.mult)
+            else:
+                nc.vector.tensor_tensor(term_a[:, t, :], sg3[:, t, :], a_bank[t][:], ALU.mult)
         out_rows = out_0.rearrange("(p t) j -> p t j", t=PACK)
         out_words = out_1[0].rearrange("p c r -> p (c r)").bitcast(I32)
         for h in range(2):
             cols = slice(h * HALF, (h + 1) * HALF)
-            for t in range(PACK):
+            for t in (0, 2, 1, 3):
                 col = slice(t, t + 1)
                 nc.scalar.activation(sg2[:, t, cols], a_win[t][:].indirect(n5_l[:, h * HALF // 16 : (h + 1) * HALF // 16]), ACT.Sigmoid, bias=bias2[:, col], scale=sl2_v[:, col])
-                nc.vector.tensor_tensor(term_b[:, t, cols], sg2[:, t, cols], b_win[t][:, cols], ALU.mult)
+                nc.vector.scalar_tensor_tensor(term_b[:, t, cols], b_bank[t][:, cols], 0.0625, sg2[:, t, cols], ALU.mult, ALU.mult)
             nc.vector.tensor_tensor(result[:, :, cols], term_a[:, :, cols], term_b[:, :, cols], ALU.add)
             nc.sync.dma_start(out_rows[:, :, cols], result[:, :, cols])
-            nc.vector.tensor_copy(woven_view(out_woven, h), planes_view(result, h))
+        nc.scalar.copy(woven_view(out_woven, 0), planes_view(result, 0))
+        nc.vector.tensor_copy(woven_view(out_woven, 1), planes_view(result, 1))
+        for h in range(2):
+            cols = slice(h * HALF, (h + 1) * HALF)
             quantise(out_w, out_s, out_woven, h)
             nc.sync.dma_start(out_words[:, cols], out_w[:, cols].bitcast(I32))
         for q in range(4):

@@ -66,11 +66,11 @@ def tile_picked_fkcdcxbgdifebl_none_po_kernel(
         def dealt_write(ap):
             return ap.rearrange("p (t m) -> p m t", t=PACK)
 
-        def planes_view(quad, h):
-            return quad[:, :, h * HALF : (h + 1) * HALF].rearrange("p t (c i) -> p c t i", i=2)
+        def planes_view(quad, first, count):
+            return quad[:, :, first : first + count].rearrange("p t (c i) -> p c t i", i=2)
 
-        def woven_view(woven, h):
-            return woven[:, h * PACK * HALF : (h + 1) * PACK * HALF].rearrange("p (c i t) -> p c t i", i=2, t=PACK)
+        def woven_view(woven, first, count):
+            return woven[:, PACK * first : PACK * (first + count)].rearrange("p (c i t) -> p c t i", i=2, t=PACK)
 
         def quantise(codes, scales, woven, h):
             cols = slice(h * HALF, (h + 1) * HALF)
@@ -84,14 +84,14 @@ def tile_picked_fkcdcxbgdifebl_none_po_kernel(
             )
 
         offs_l = load_list("offs_l", offs)
-        w1_w = load_words(nc.scalar, "w1_w", "w_words", w1_words, S)
         n4_l = load_list("n4_l", n4)
         n3_l = load_list("n3_l", n3)
         n2_l = load_list("n2_l", n2)
         n1_l = load_list("n1_l", n1)
-        x_w = load_words(nc.sync, "x_w", "x_words", x_words, T)
-        cand_l = load_list("cand_l", cand)
         n6_l = load_list("n6_l", n6)
+        x_w = load_words(nc.sync, "x_w", "x_words", x_words, T)
+        w1_w = load_words(nc.sync, "w1_w", "w_words", w1_words, S)
+        cand_l = load_list("cand_l", cand)
         n5_l = load_list("n5_l", n5)
         x_s = load_scales(nc.scalar, nc.vector, "x_s", x_scales, T)
         w2_s = load_scales(nc.sync, nc.vector, "w2_s", w2_scales, S)
@@ -99,22 +99,25 @@ def tile_picked_fkcdcxbgdifebl_none_po_kernel(
         sl_v = load_rows(nc.gpsimd, "sl_v", "slope", sl)
         th_v = load_rows(nc.gpsimd, "th_v", "threshold", th)
         gs_v = load_rows(nc.gpsimd, "gs_v", "weight", gs)
-        gn_v = load_rows(nc.gpsimd, "gn_v", "gain", gn)
 
         pick_s = keep.tile([P, S], U8, name="pick_s", align_bytes=64)
         nc.vector.tensor_copy(pick_s[:], x_s[:].indirect(offs_l[:]))
-        w1_sd = keep.tile([P, S], U8, name="w1_sd", tag="w_sd", align_bytes=64)
+        w1_sd = keep.tile([P, S], U8, name="w1_sd", align_bytes=64)
         for t in range(PACK):
             nc.gpsimd.tensor_copy(dealt_tile(w1_sd[:])[:, t, :], dealt_read(w1_s[:])[:, t, :])
         w1_wd = keep.tile([P, S], U32, name="w1_wd", align_bytes=64)
-        nc.scalar.copy(dealt_tile(w1_wd[:]), dealt_read(w1_w[:].bitcast(U32)))
+        for ts in (slice(0, 1), slice(1, PACK)):
+            nc.scalar.copy(dealt_tile(w1_wd[:])[:, ts, :], dealt_read(w1_w[:].bitcast(U32))[:, ts, :])
         w2_w = load_words(nc.sync, "w2_w", "w_words", w2_words, S)
         neg_th = keep.tile([P, PACK], F32, name="neg_th")
         nc.gpsimd.tensor_scalar(neg_th[:], th_v[:], -1.0, 0.0, ALU.mult, ALU.add)
         bias1 = keep.tile([P, PACK], F32, name="bias1")
         nc.gpsimd.tensor_tensor(bias1[:], neg_th[:], sl_v[:], ALU.mult)
+        neg_gs = keep.tile([P, PACK], F32, name="neg_gs")
+        nc.gpsimd.tensor_scalar(neg_gs[:], gs_v[:], -1.0, 0.0, ALU.mult, ALU.add)
+        gn_v = load_rows(nc.sync, "gn_v", "threshold", gn)
         neg_gn = keep.tile([P, PACK], F32, name="neg_gn")
-        nc.gpsimd.tensor_scalar(neg_gn[:], gn_v[:], -1.0, 0.0, ALU.mult, ALU.add)
+        nc.vector.tensor_scalar(neg_gn[:], gn_v[:], -1.0, 0.0, ALU.mult, ALU.add)
         pick_w = keep.tile([P, S], U32, name="pick_w", align_bytes=64)
         nc.vector.tensor_copy(pick_w[:], x_w[:].bitcast(U32).indirect(offs_l[:]))
         cand_s = keep.tile([P, S], U8, name="cand_s", align_bytes=64)
@@ -136,7 +139,7 @@ def tile_picked_fkcdcxbgdifebl_none_po_kernel(
             nc.scalar.activation(y_win[t][:, 0:S], y_bank[t][:], ACT.Copy)
             nc.sync.dma_start(y_plain[t][:], y_win[t][:, 0:S])
             nc.scalar.activation(sg[:, t, :], y_win[t][:].indirect(n4_l[:]), ACT.Sigmoid, bias=bias1[:, col], scale=sl_v[:, col])
-            nc.vector.tensor_scalar(keep_pa[:, t, :], sg[:, t, :], 1.0, gs_v[:, col], ALU.subtract, ALU.mult)
+            nc.gpsimd.tensor_scalar(keep_pa[:, t, :], sg[:, t, :], gs_v[:, col], neg_gs[:, col], ALU.mult, ALU.add)
             nc.vector.scalar_tensor_tensor(from_y[:, t, :], sg[:, t, :], gs_v[:, col], y_bank[t][:], ALU.mult, ALU.mult)
             nc.vector.tensor_tensor(from_pa[:, t, :], y_win[t][:].indirect(n3_l[:]), keep_pa[:, t, :], ALU.mult)
         sl3_v = load_rows(nc.sync, "sl3_v", "slope", sl3)
@@ -150,7 +153,7 @@ def tile_picked_fkcdcxbgdifebl_none_po_kernel(
         z2_s = keep.tile([P, S], U8, name="z2_s", align_bytes=64)
         b_bank = [psum.tile([P, S], F32, name="b_bank%d" % t) for t in range(PACK)]
         for h in range(2):
-            nc.vector.tensor_tensor(woven_view(z2_woven, h), planes_view(from_y, h), planes_view(from_pa, h), ALU.subtract)
+            nc.vector.tensor_tensor(woven_view(z2_woven, h * HALF, HALF), planes_view(from_y, h * HALF, HALF), planes_view(from_pa, h * HALF, HALF), ALU.subtract)
         for h in range(2):
             quantise(z2_w, z2_s, z2_woven, h)
             for t in range(PACK):
@@ -163,10 +166,10 @@ def tile_picked_fkcdcxbgdifebl_none_po_kernel(
             nc.scalar.activation(gate[:, t, :], y_win[t][:].indirect(n2_l[:]), ACT.Sigmoid)
         for t in range(PACK):
             nc.scalar.activation(gain[:, t, :], gate[:, t, :], ACT.Copy, scale=neg_gn[:, t : t + 1])
+        w2_sd = keep.tile([P, S], U8, name="w2_sd", align_bytes=64)
+        nc.gpsimd.tensor_copy(dealt_tile(w2_sd[:]), dealt_read(w2_s[:]))
         w2_wd = keep.tile([P, S], U32, name="w2_wd", align_bytes=64)
-        nc.gpsimd.tensor_copy(dealt_tile(w2_wd[:]), dealt_read(w2_w[:].bitcast(U32)))
-        w2_sd = keep.tile([P, S], U8, name="w2_sd", tag="w_sd", align_bytes=64)
-        nc.vector.tensor_copy(dealt_tile(w2_sd[:]), dealt_read(w2_s[:]))
+        nc.vector.tensor_copy(dealt_tile(w2_wd[:]), dealt_read(w2_w[:].bitcast(U32)))
         for t in range(PACK):
             nc.vector.tensor_tensor(diff[:, t, :], y_win[t][:].indirect(n1_l[:]), y_plain[t][:], ALU.subtract)
         z_woven = keep.tile([P, PACK * S], BF16, name="z_woven", align_bytes=64)
@@ -174,7 +177,7 @@ def tile_picked_fkcdcxbgdifebl_none_po_kernel(
         z_s = keep.tile([P, S], U8, name="z_s", align_bytes=64)
         a_bank = [psum.tile([P, S], F32, name="a_bank%d" % t, tag="first%d" % t) for t in range(PACK)]
         for h in range(2):
-            nc.vector.tensor_tensor(woven_view(z_woven, h), planes_view(diff, h), planes_view(gain, h), ALU.mult)
+            nc.vector.tensor_tensor(woven_view(z_woven, h * HALF, HALF), planes_view(diff, h * HALF, HALF), planes_view(gain, h * HALF, HALF), ALU.mult)
         for h in range(2):
             quantise(z_w, z_s, z_woven, h)
             for t in range(PACK):
@@ -215,8 +218,10 @@ def tile_picked_fkcdcxbgdifebl_none_po_kernel(
                 nc.vector.scalar_tensor_tensor(term_b[:, t, cols], b_bank[t][:, cols], 0.0625, sg2[:, t, cols], ALU.mult, ALU.mult)
             nc.vector.tensor_tensor(result[:, :, cols], term_a[:, :, cols], term_b[:, :, cols], ALU.add)
             nc.sync.dma_start(out_rows[:, :, cols], result[:, :, cols])
-        nc.scalar.copy(woven_view(out_woven, 0), planes_view(result, 0))
-        nc.vector.tensor_copy(woven_view(out_woven, 1), planes_view(result, 1))
+        quarter = HALF // 2
+        nc.scalar.copy(woven_view(out_woven, 0, HALF), planes_view(result, 0, HALF))
+        nc.scalar.copy(woven_view(out_woven, HALF, quarter), planes_view(result, HALF, quarter))
+        nc.vector.tensor_copy(woven_view(out_woven, S - quarter, quarter), planes_view(result, S - quarter, quarter))
         for h in range(2):
             cols = slice(h * HALF, (h + 1) * HALF)
             quantise(out_w, out_s, out_woven, h)

@@ -96,6 +96,10 @@ def tile_picked_fkcdcxbgdifebl_none_po_kernel(
         x_s = load_scales(nc.scalar, nc.vector, "x_s", x_scales, T)
         w2_s = load_scales(nc.sync, nc.vector, "w2_s", w2_scales, S)
         w1_s = load_scales(nc.scalar, nc.vector, "w1_s", w1_scales, S)
+        warm_in = keep.tile([P, 1], F32, name="warm_in")
+        warm_out = keep.tile([P, 1], F32, name="warm_out")
+        nc.vector.memset(warm_in[:], 0.0)
+        nc.scalar.activation(warm_out[:], warm_in[:], ACT.Sigmoid)
         sl_v = load_rows(nc.gpsimd, "sl_v", "slope", sl)
         th_v = load_rows(nc.gpsimd, "th_v", "threshold", th)
         gs_v = load_rows(nc.gpsimd, "gs_v", "weight", gs)

from contextlib import ExitStack

import concourse.mybir as mybir

K, T, S = 512, 2048, 512
FLOPS = 3 * 2 * K * S * S

F32 = mybir.dt.float32
BF16 = mybir.dt.bfloat16
I32 = mybir.dt.int32
U32 = mybir.dt.uint32
U16 = mybir.dt.uint16
U8 = mybir.dt.uint8
FP8X4 = mybir.dt.float8_e4m3fn_x4
ALU = mybir.AluOpType
ACT = mybir.ActivationFunctionType

P = 128
PACK = 4
HALF = S // 2
WINDOW = 2 * S


def tile_picked_fkcdcxbgdifebl_none_po_kernel(
    tc, x_words, x_scales, w1_words, w1_scales, sl, th, gn, w2_words, w2_scales, gs, sl2, th2, sl3, th3,
    offs, n1, n2, n3, n4, cand, n5, n6, out_0, out_1, out_2,
):
    nc = tc.nc
    with ExitStack() as ctx:
        keep = ctx.enter_context(tc.tile_pool(name="keep", bufs=1))
        psum = ctx.enter_context(tc.psum_pool(name="psum", bufs=1))

        def load_list(name, src):
            lst = keep.tile([P, S // 16], U16, name=name)
            nc.sync.dma_start(lst[:], src)
            return lst

        def load_words(queue, name, tag, src, width):
            words = keep.tile([P, width], I32, name=name, tag=tag, align_bytes=64)
            queue.dma_start(words[:], src[0].rearrange("p c r -> p (c r)").bitcast(I32))
            return words

        def load_scales(queue, zeroing, name, src, width):
            plane = keep.tile([P, width], U8, name=name, align_bytes=64)
            zeroing.memset(plane[:].bitcast(I32), 0)
            for q in range(4):
                queue.dma_start(plane[32 * q : 32 * q + 4, :].bitcast(I32), src[0, 4 * q : 4 * q + 4, :].bitcast(I32))
            return plane

        def load_rows(queue, name, tag, src):
            vec = keep.tile([P, PACK], F32, name=name, tag=tag)
            queue.dma_start(vec[:], src.rearrange("(p t) o -> p (t o)", t=PACK))
            return vec

        def negated_product(name, u, v):
            neg = keep.tile([P, PACK], F32, name=name)
            nc.vector.scalar_tensor_tensor(neg[:], u[:], -1.0, v[:], ALU.mult, ALU.mult)
            return neg

        def dealt_read(ap):
            return ap.rearrange("p (m t) -> p t m", t=PACK)

        def dealt_tile(ap):
            return ap.rearrange("p (t m) -> p t m", t=PACK)

        def dealt_write(ap):
            return ap.rearrange("p (t m) -> p m t", t=PACK)

        def planes_view(quad, first, count):
            return quad[:, :, first : first + count].rearrange("p t (c i) -> p c t i", i=2)

        def woven_view(woven, first, count):
            return woven[:, PACK * first : PACK * (first + count)].rearrange("p (c i t) -> p c t i", i=2, t=PACK)

        def quantise(codes, scales, woven, h):
            cols = slice(h * HALF, (h + 1) * HALF)
            nc.vector.quantize_mx(out=codes[:, cols].bitcast(FP8X4), scales=scales[:, cols], in_=woven[:, h * PACK * HALF : (h + 1) * PACK * HALF])

        def product(bank, lhs_codes, lhs_scales, t, rhs_codes, rhs_scales, cols):
            rows = slice(t * P, (t + 1) * P)
            nc.tensor.matmul_mx(
                out=bank[:, cols], lhsT=lhs_codes[:, rows].bitcast(FP8X4), lhsT_scale=lhs_scales[:, rows],
                rhs=rhs_codes[:, cols].bitcast(FP8X4), rhs_scale=rhs_scales[:, cols], start=True, stop=True,
            )

        offs_l = load_list("offs_l", offs)
        n4_l = load_list("n4_l", n4)
        n3_l = load_list("n3_l", n3)
        n2_l = load_list("n2_l", n2)
        n1_l = load_list("n1_l", n1)
        n6_l = load_list("n6_l", n6)
        x_w = load_words(nc.sync, "x_w", "x_words", x_words, T)
        w1_w = load_words(nc.sync, "w1_w", "w_words", w1_words, S)
        cand_l = load_list("cand_l", cand)
        n5_l = load_list("n5_l", n5)
        x_s = load_scales(nc.scalar, nc.vector, "x_s", x_scales, T)
        w2_s = load_scales(nc.sync, nc.vector, "w2_s", w2_scales, S)
        w1_s = load_scales(nc.scalar, nc.vector, "w1_s", w1_scales, S)
        warm_in = keep.tile([P, 1], F32, name="warm_in")
        warm_out = keep.tile([P, 1], F32, name="warm_out")
        nc.vector.memset(warm_in[:], 0.0)
        nc.scalar.activation(warm_out[:], warm_in[:], ACT.Sigmoid)
        sl_v = load_rows(nc.gpsimd, "sl_v", "slope", sl)
        th_v = load_rows(nc.gpsimd, "th_v", "threshold", th)
        gs_v = load_rows(nc.gpsimd, "gs_v", "weight", gs)

        pick_s = keep.tile([P, S], U8, name="pick_s", align_bytes=64)
        nc.vector.tensor_copy(pick_s[:], x_s[:].indirect(offs_l[:]))
        w1_sd = keep.tile([P, S], U8, name="w1_sd", align_bytes=64)
        for t in range(PACK):
            nc.gpsimd.tensor_copy(dealt_tile(w1_sd[:])[:, t, :], dealt_read(w1_s[:])[:, t, :])
        w1_wd = keep.tile([P, S], U32, name="w1_wd", align_bytes=64)
        for ts in (slice(0, 1), slice(1, PACK)):
            nc.scalar.copy(dealt_tile(w1_wd[:])[:, ts, :], dealt_read(w1_w[:].bitcast(U32))[:, ts, :])
        w2_w = load_words(nc.sync, "w2_w", "w_words", w2_words, S)
        neg_th = keep.tile([P, PACK], F32, name="neg_th")
        nc.gpsimd.tensor_scalar(neg_th[:], th_v[:], -1.0, 0.0, ALU.mult, ALU.add)
        bias1 = keep.tile([P, PACK], F32, name="bias1")
        nc.gpsimd.tensor_tensor(bias1[:], neg_th[:], sl_v[:], ALU.mult)
        neg_gs = keep.tile([P, PACK], F32, name="neg_gs")
        nc.gpsimd.tensor_scalar(neg_gs[:], gs_v[:], -1.0, 0.0, ALU.mult, ALU.add)
        gn_v = load_rows(nc.sync, "gn_v", "threshold", gn)
        neg_gn = keep.tile([P, PACK], F32, name="neg_gn")
        nc.vector.tensor_scalar(neg_gn[:], gn_v[:], -1.0, 0.0, ALU.mult, ALU.add)
        pick_w = keep.tile([P, S], U32, name="pick_w", align_bytes=64)
        nc.vector.tensor_copy(pick_w[:], x_w[:].bitcast(U32).indirect(offs_l[:]))
        cand_s = keep.tile([P, S], U8, name="cand_s", align_bytes=64)
        nc.vector.tensor_copy(dealt_write(cand_s[:]), x_s[:].indirect(cand_l[:]))
        cand_w = keep.tile([P, S], U32, name="cand_w", align_bytes=64)
        nc.vector.tensor_copy(dealt_write(cand_w[:]), x_w[:].bitcast(U32).indirect(cand_l[:]))

        y_bank = [psum.tile([P, S], F32, name="y_bank%d" % t, tag="first%d" % t) for t in range(PACK)]
        y_win = [keep.tile([P, WINDOW], F32, name="y_win%d" % t) for t in range(PACK)]
        y_plain = [keep.tile([P, S], F32, name="y_plain%d" % t) for t in range(PACK)]
        sg = keep.tile([P, PACK, S], F32, name="sg")
        keep_pa = keep.tile([P, PACK, S], F32, name="keep_pa")
        from_pa = keep.tile([P, PACK, S], F32, name="from_pa", tag="gathered")
        from_y = keep.tile([P, PACK, S], F32, name="from_y")
        for t in range(PACK):
            product(y_bank[t], w1_wd, w1_sd, t, pick_w, pick_s, slice(0, S))
        for t in range(PACK):
            col = slice(t, t + 1)
            nc.scalar.activation(y_win[t][:, 0:S], y_bank[t][:], ACT.Copy)
            nc.sync.dma_start(y_plain[t][:], y_win[t][:, 0:S])
            nc.scalar.activation(sg[:, t, :], y_win[t][:].indirect(n4_l[:]), ACT.Sigmoid, bias=bias1[:, col], scale=sl_v[:, col])
            nc.gpsimd.tensor_scalar(keep_pa[:, t, :], sg[:, t, :], gs_v[:, col], neg_gs[:, col], ALU.mult, ALU.add)
            nc.vector.scalar_tensor_tensor(from_y[:, t, :], sg[:, t, :], gs_v[:, col], y_bank[t][:], ALU.mult, ALU.mult)
            nc.vector.tensor_tensor(from_pa[:, t, :], y_win[t][:].indirect(n3_l[:]), keep_pa[:, t, :], ALU.mult)
        sl3_v = load_rows(nc.sync, "sl3_v", "slope", sl3)
        th3_v = load_rows(nc.sync, "th3_v", "threshold", th3)
        bias3 = negated_product("bias3", sl3_v, th3_v)
        sl2_v = load_rows(nc.sync, "sl2_v", "weight", sl2)
        th2_v = load_rows(nc.sync, "th2_v", "threshold", th2)
        bias2 = negated_product("bias2", sl2_v, th2_v)
        z2_woven = keep.tile([P, PACK * S], BF16, name="z2_woven", align_bytes=64)
        z2_w = keep.tile([P, S], U32, name="z2_w", align_bytes=64)
        z2_s = keep.tile([P, S], U8, name="z2_s", align_bytes=64)
        b_bank = [psum.tile([P, S], F32, name="b_bank%d" % t) for t in range(PACK)]
        for h in range(2):
            nc.vector.tensor_tensor(woven_view(z2_woven, h * HALF, HALF), planes_view(from_y, h * HALF, HALF), planes_view(from_pa, h * HALF, HALF), ALU.subtract)
        for h in range(2):
            quantise(z2_w, z2_s, z2_woven, h)
            for t in range(PACK):
                product(b_bank[t], cand_w, cand_s, t, z2_w, z2_s, slice(h * HALF, (h + 1) * HALF))

        gate = keep.tile([P, PACK, S], F32, name="gate")
        gain = keep.tile([P, PACK, S], F32, name="gain")
        diff = keep.tile([P, PACK, S], F32, name="diff", tag="gathered")
        for t in range(PACK):
            nc.scalar.activation(gate[:, t, :], y_win[t][:].indirect(n2_l[:]), ACT.Sigmoid)
        for t in range(PACK):
            nc.scalar.activation(gain[:, t, :], gate[:, t, :], ACT.Copy, scale=neg_gn[:, t : t + 1])
        w2_sd = keep.tile([P, S], U8, name="w2_sd", align_bytes=64)
        nc.gpsimd.tensor_copy(dealt_tile(w2_sd[:]), dealt_read(w2_s[:]))
        w2_wd = keep.tile([P, S], U32, name="w2_wd", align_bytes=64)
        nc.vector.tensor_copy(dealt_tile(w2_wd[:]), dealt_read(w2_w[:].bitcast(U32)))
        for t in range(PACK):
            nc.vector.tensor_tensor(diff[:, t, :], y_win[t][:].indirect(n1_l[:]), y_plain[t][:], ALU.subtract)
        z_woven = keep.tile([P, PACK * S], BF16, name="z_woven", align_bytes=64)
        z_w = keep.tile([P, S], U32, name="z_w", align_bytes=64)
        z_s = keep.tile([P, S], U8, name="z_s", align_bytes=64)
        a_bank = [psum.tile([P, S], F32, name="a_bank%d" % t, tag="first%d" % t) for t in range(PACK)]
        for h in range(2):
            nc.vector.tensor_tensor(woven_view(z_woven, h * HALF, HALF), planes_view(diff, h * HALF, HALF), planes_view(gain, h * HALF, HALF), ALU.mult)
        for h in range(2):
            quantise(z_w, z_s, z_woven, h)
            for t in range(PACK):
                product(a_bank[t], w2_wd, w2_sd, t, z_w, z_s, slice(h * HALF, (h + 1) * HALF))

        b_win = [keep.tile([P, WINDOW], F32, name="b_win%d" % t) for t in range(PACK)]
        sg3 = keep.tile([P, PACK, S], F32, name="sg3")
        for t in range(PACK):
            col = slice(t, t + 1)
            nc.scalar.activation(b_win[t][:, 0:S], b_bank[t][:], ACT.Copy, scale=0.0625)
            nc.scalar.activation(sg3[:, t, :], b_win[t][:].indirect(n6_l[:]), ACT.Sigmoid, bias=bias3[:, col], scale=sl3_v[:, col])

        a_win = [keep.tile([P, WINDOW], F32, name="a_win%d" % t) for t in range(PACK)]
        sg2 = keep.tile([P, PACK, S], F32, name="sg2")
        term_a = keep.tile([P, PACK, S], F32, name="term_a")
        term_b = keep.tile([P, PACK, S], F32, name="term_b")
        result = keep.tile([P, PACK, S], F32, name="result")
        out_woven = keep.tile([P, PACK * S], BF16, name="out_woven", align_bytes=64)
        out_w = keep.tile([P, S], U32, name="out_w", align_bytes=64)
        out_s = keep.tile([P, S], U8, name="out_s", align_bytes=64)
        for t in range(PACK):
            if t % 2 == 0:
                nc.scalar.activation(a_win[t][:, 0:S], a_bank[t][:], ACT.Copy)
            else:
                nc.vector.tensor_copy(a_win[t][:, 0:S], a_bank[t][:])
        for t in range(PACK):
            if t % 2 == 0:
                nc.gpsimd.tensor_tensor(term_a[:, t, :], sg3[:, t, :], a_win[t][:, 0:S], ALU.mult)
            else:
                nc.vector.tensor_tensor(term_a[:, t, :], sg3[:, t, :], a_bank[t][:], ALU.mult)
        out_rows = out_0.rearrange("(p t) j -> p t j", t=PACK)
        out_words = out_1[0].rearrange("p c r -> p (c r)").bitcast(I32)
        for h in range(2):
            cols = slice(h * HALF, (h + 1) * HALF)
            for t in (0, 2, 1, 3):
                col = slice(t, t + 1)
                nc.scalar.activation(sg2[:, t, cols], a_win[t][:].indirect(n5_l[:, h * HALF // 16 : (h + 1) * HALF // 16]), ACT.Sigmoid, bias=bias2[:, col], scale=sl2_v[:, col])
                nc.vector.scalar_tensor_tensor(term_b[:, t, cols], b_bank[t][:, cols], 0.0625, sg2[:, t, cols], ALU.mult, ALU.mult)
            nc.vector.tensor_tensor(result[:, :, cols], term_a[:, :, cols], term_b[:, :, cols], ALU.add)
            nc.sync.dma_start(out_rows[:, :, cols], result[:, :, cols])
        quarter = HALF // 2
        nc.scalar.copy(woven_view(out_woven, 0, HALF), planes_view(result, 0, HALF))
        nc.scalar.copy(woven_view(out_woven, HALF, quarter), planes_view(result, HALF, quarter))
        nc.vector.tensor_copy(woven_view(out_woven, S - quarter, quarter), planes_view(result, S - quarter, quarter))
        for h in range(2):
            cols = slice(h * HALF, (h + 1) * HALF)
            quantise(out_w, out_s, out_woven, h)
            nc.sync.dma_start(out_words[:, cols], out_w[:, cols].bitcast(I32))
        for q in range(4):
            queue = nc.sync if q % 2 == 0 else nc.scalar
            queue.dma_start(out_2[0, 4 * q : 4 * q + 4, :].bitcast(I32), out_s[32 * q : 32 * q + 4, :].bitcast(I32))
